import numpy as np
import ml_dtypes


def mxq(x, axis, fmt="e4m3"):
    dtype, down = {"e4m3": (ml_dtypes.float8_e4m3fn, 7), "e5m2": (ml_dtypes.float8_e5m2, 14)}[fmt]
    v = np.moveaxis(np.asarray(x, np.float32).astype(ml_dtypes.bfloat16).astype(np.float64), axis, -1)
    blocks = v.reshape(v.shape[:-1] + (-1, 32))
    amax = np.abs(blocks).max(-1, keepdims=True)
    byte = np.maximum(np.where(amax > 0, np.frexp(amax)[1] - 1 + 127, 0) - down, 1)
    scale = np.exp2(byte - 127.0)
    codes = (blocks / scale).astype(np.float32).astype(dtype).astype(np.float64)
    return np.moveaxis((codes * scale).reshape(v.shape), -1, axis)


WIDE = False


def mx_kscale(k):
    if not WIDE:
        return np.ones(k)
    levels = np.array([10, -10, 5, -5, 0])
    if k % 512:
        return np.exp2(np.random.permutation(np.resize(levels, k // 32))).repeat(32)
    a = np.empty((k // 512, 16))
    for p in range(k // 512):
        a[p, :8] = np.random.permutation(np.resize(levels, 8))
        for g in range(8):
            far = levels[np.abs(levels - a[p, g]) >= 10]
            a[p, g + 8] = far[np.random.randint(len(far))]
    return np.exp2(a.ravel()).repeat(32)


def f64(x):
    return np.asarray(x).astype(np.float64)


def striped(idx):
    return np.tile(np.asarray(idx).reshape(-1, 16).T, (8, 1)).astype(np.uint16)


def unstriped(offs):
    return offs[:16].T.reshape(-1).astype(np.int64)


E2M1 = np.array([0.0, 0.5, 1.0, 1.5, 2.0, 3.0, 4.0, 6.0, -0.0, -0.5, -1.0, -1.5, -2.0, -3.0, -4.0, -6.0])


def pack_weight(w, fmt):
    k, n = w.shape
    w = f64(np.asarray(w, np.float32).astype(ml_dtypes.bfloat16)).reshape(k // 32, 32, n)
    amax = np.abs(w).max(1)
    if fmt == "e4m3":
        byte = np.frexp(amax)[1] - 1 + 127 - 7
    else:
        mant, ex = np.frexp(amax / 6.0)
        byte = np.where(mant > 0.5, ex, ex - 1) + 127
    byte = np.clip(np.where(amax > 0, byte, 1), 1, 254)
    scaled = (w * np.exp2(127.0 - byte)[:, None, :]).reshape(k, n).astype(np.float32)
    by_word = np.ascontiguousarray(scaled.reshape(k // 512, 128, 4, n).transpose(0, 1, 3, 2))
    if fmt == "e4m3":
        words = by_word.astype(ml_dtypes.float8_e4m3fn).view(np.uint8)
    else:
        c = by_word.astype(ml_dtypes.float4_e2m1fn).view(np.uint8) & 0xF
        words = (c[..., 0::2] | (c[..., 1::2] << 4)).reshape(k // 512, 128, 2 * n)
    return np.ascontiguousarray(words), np.ascontiguousarray(byte.astype(np.uint8).reshape(k // 512, 16, n))


def unpack_weight(words, scales, fmt):
    g, _, n = scales.shape
    words = np.ascontiguousarray(words).reshape(g, 128, n, -1)
    if fmt == "e4m3":
        vals = words.view(ml_dtypes.float8_e4m3fn).astype(np.float64)
    else:
        nib = np.empty((g, 128, n, 4), np.uint8)
        nib[..., 0::2] = words & 0xF
        nib[..., 1::2] = words >> 4
        vals = E2M1[nib]
    vals = vals * np.repeat(np.exp2(scales.astype(np.float64) - 127.0), 8, axis=1)[..., None]
    return vals.transpose(0, 1, 3, 2).reshape(g * 512, n)


def softplus(v):
    return np.log(1.0 + np.exp(v))


def silu(v):
    return v / (1.0 + np.exp(-v))


D, K, R, T, I, Q, G = 512, 512, 512, 2048, 512, 128, 32


def setup_inputs():
    n = np.random.standard_normal
    idx = np.random.permutation(T)[:I]
    fd = mx_kscale(D)
    fk = mx_kscale(K)
    fi = mx_kscale(I)
    keysp = pack_weight(n((D, T)) / fd[:, None], "e4m3")
    tabp = pack_weight(n((K, T)) / fk[:, None], "e4m3")
    return {
        "query": (n((D, Q)) * 0.9 / np.sqrt(D) * fd[:, None]).astype(np.float32),
        "keys_words": keysp[0],
        "keys_scales": keysp[1],
        "th": (np.random.uniform(-0.3, 0.6, (Q, 1))).astype(np.float32),
        "reserve": (np.random.uniform(50.0, 200.0, (Q, 1))).astype(np.float32),
        "tab_words": tabp[0],
        "tab_scales": tabp[1],
        "w1": (n((K, R)) * 1 / np.sqrt(K) * fk[:, None]).astype(np.float32),
        "gain": (np.random.uniform(0.7, 2.0, (R, 1))).astype(np.float32),
        "os": (np.random.uniform(4.0, 16.0, (1, I)) * fi).astype(np.float32),
        "vs": (np.random.uniform(0.5, 2.0, (1, I)) / fi).astype(np.float32),
        "offs": striped(idx),
    }


def reference(query, keys_words, keys_scales, th, reserve, tab_words, tab_scales, w1, gain, os, vs, offs):
    idx = unstriped(offs)
    keysu = unpack_weight(keys_words, keys_scales, "e4m3")
    tabu = unpack_weight(tab_words, tab_scales, "e4m3")
    queryq = mxq(f64(query), 0, "e4m3")
    keysidxg = keysu[:, idx]
    a = queryq.T @ keysidxg
    p = softplus(a - f64(th))
    z = np.sum(p, axis=1, keepdims=True) + f64(reserve)
    w = p / z
    w1q = mxq(f64(w1), 0, "e4m3")
    tabidxg = tabu[:, idx]
    zh = w1q.T @ tabidxg
    mz = np.sqrt(np.square(zh).reshape(R, G, I // G).mean(axis=2) + 0.1)
    mzr = np.repeat(mz, I // G, axis=1)
    hv = silu(zh / mzr * f64(gain))
    wo1 = w * f64(os)
    wt1 = wo1.T
    hw = hv * f64(vs)
    ht1 = hw.T
    wt1q = mxq(wt1, 0, "e4m3")
    ht1q = mxq(ht1, 0, "e4m3")
    o = wt1q.T @ ht1q
    return o

@@ -1,0 +1,196 @@
+from contextlib import ExitStack
+
+import concourse.mybir as mybir
+from concourse.masks import make_identity
+
+D, K, R, T, I, Q, G = 512, 512, 512, 2048, 512, 128, 32
+FLOPS = 2 * (D * Q * I + K * R * I + I * Q * R)
+
+F32 = mybir.dt.float32
+BF16 = mybir.dt.bfloat16
+I32 = mybir.dt.int32
+U32 = mybir.dt.uint32
+U16 = mybir.dt.uint16
+U8 = mybir.dt.uint8
+FP8X4 = mybir.dt.float8_e4m3fn_x4
+ALU = mybir.AluOpType
+ACT = mybir.ActivationFunctionType
+AX = mybir.AxisListType
+
+P = 128
+PACK = 4
+BLOCKS = R // P
+PAGE = I // G
+EXP_CAP = 2.0**40
+
+
+def tile_attend_lrscaled_capped_kernel(
+    tc, query, keys_words, keys_scales, th, reserve, tab_words, tab_scales, w1, gain, slot_os, slot_vs, offs, out
+):
+    nc = tc.nc
+    with ExitStack() as ctx:
+        sb = ctx.enter_context(tc.tile_pool(name="sb", bufs=1))
+        ps = ctx.enter_context(tc.psum_pool(name="ps", bufs=1))
+
+        def alloc(name, shape, dtype):
+            return sb.tile(shape, dtype, name=name, align_bytes=64)
+
+        def quantize(name, grouped, width):
+            codes = alloc(name + "_codes", [P, width], U32)
+            scales = alloc(name + "_scales", [P, width], U8)
+            nc.vector.quantize_mx(out=codes[:].bitcast(FP8X4), scales=scales[:], in_=grouped)
+            return codes, scales
+
+        def load_scale_rows(queue, pool_tile, scales_hbm, j):
+            queue.dma_start(out=pool_tile[j:P:32, :].bitcast(I32), in_=scales_hbm[0, j:16:4, :].bitcast(I32))
+
+        keys_bytes = alloc("keys_bytes", [P, T], U8)
+        nc.gpsimd.memset(keys_bytes[:].bitcast(I32), 0)
+        tab_bytes = alloc("tab_bytes", [P, T], U8)
+        nc.vector.memset(tab_bytes[:].bitcast(I32), 0)
+        for j in range(4):
+            load_scale_rows(nc.scalar if j < 3 else nc.gpsimd, keys_bytes, keys_scales, j)
+        for j in range(4):
+            load_scale_rows(nc.gpsimd, tab_bytes, tab_scales, j)
+        th_col = alloc("th_col", [P, 1], F32)
+        nc.scalar.dma_start(out=th_col[:], in_=th)
+
+        offsets = alloc("offsets", [P, I // 16], U16)
+        nc.sync.dma_start(offsets[:], offs)
+        q_raw = alloc("q_raw", [P, PACK, Q], F32)
+        nc.sync.dma_start(out=q_raw[:], in_=query.rearrange("(p j) q -> p j q", j=PACK))
+        keys_pool = alloc("keys_pool", [P, T], I32)
+        nc.sync.dma_start(out=keys_pool[:], in_=keys_words[0].rearrange("p n t -> p (n t)").bitcast(I32))
+        tab_pool = alloc("tab_pool", [P, T], I32)
+        nc.sync.dma_start(out=tab_pool[:], in_=tab_words[0].rearrange("p n t -> p (n t)").bitcast(I32))
+        w1_rows = w1.rearrange("(p j) r -> p j r", j=PACK)
+        w_raw = []
+        for h in range(2):
+            half = alloc(f"w_raw{h}", [P, PACK, 2 * P], F32)
+            nc.sync.dma_start(out=half[:], in_=w1_rows[:, :, 2 * P * h : 2 * P * (h + 1)])
+            w_raw.append(half)
+        reserve_col = alloc("reserve_col", [P, 1], F32)
+        nc.sync.dma_start(out=reserve_col[:], in_=reserve)
+        os_cols = alloc("os_cols", [P, PACK], F32)
+        nc.sync.dma_start(out=os_cols[:], in_=slot_os.rearrange("o (p t) -> p (o t)", t=PACK))
+        vs_cols = alloc("vs_cols", [P, PACK], F32)
+        nc.sync.dma_start(out=vs_cols[:], in_=slot_vs.rearrange("o (p t) -> p (o t)", t=PACK))
+        gain_cols = alloc("gain_cols", [P, BLOCKS], F32)
+        with nc.allow_non_contiguous_dma(reason="one gain a partition for each block of hidden features"):
+            nc.sync.dma_start(out=gain_cols[:], in_=gain.rearrange("(b p) o -> p (b o)", p=P))
+
+        ident = alloc("ident", [P, P], F32)
+        make_identity(nc, ident[:])
+
+        neg_th = alloc("neg_th", [P, 1], F32)
+        nc.scalar.mul(neg_th[:], th_col[:], -1.0)
+        q_grouped = alloc("q_grouped", [P, Q, PACK], BF16)
+        nc.vector.tensor_copy(out=q_grouped[:], in_=q_raw[:].rearrange("p j q -> p q j"))
+        keys_gs = alloc("keys_gs", [P, I], U8)
+        nc.vector.tensor_copy(keys_gs[:], keys_bytes[:].indirect(offsets[:]))
+        q_codes, q_scales = quantize("q", q_grouped[:].rearrange("p q j -> p (q j)"), Q)
+        keys_g = alloc("keys_g", [P, I], U32)
+        nc.vector.tensor_copy(keys_g[:], keys_pool[:].bitcast(U32).indirect(offsets[:]))
+        scores = ps.tile([P, I], F32, name="scores", tag="bank_a")
+        nc.tensor.matmul_mx(
+            out=scores[:], lhsT=q_codes[:].bitcast(FP8X4), lhsT_scale=q_scales[:],
+            rhs=keys_g[:].bitcast(FP8X4), rhs_scale=keys_gs[:], start=True, stop=True,
+        )
+        scores_dealt = scores[:].rearrange("q (p t) -> q t p", t=PACK)
+        expx = alloc("expx", [P, PACK, P], F32)
+        nc.scalar.activation(expx[:], scores_dealt, ACT.Exp, bias=neg_th[:])
+        capped = alloc("capped", [P, PACK, P], F32)
+        nc.gpsimd.tensor_scalar(capped[:], expx[:], EXP_CAP, 0.0, ALU.min, ALU.max)
+        soft = alloc("soft", [P, PACK, P], F32)
+        nc.scalar.activation(soft[:], capped[:], ACT.Ln, bias=1.0)
+
+        tab_gs = alloc("tab_gs", [P, PACK, P], U8)
+        nc.vector.tensor_copy(tab_gs[:].rearrange("k t p -> k p t"), tab_bytes[:].indirect(offsets[:]))
+        tab_g = alloc("tab_g", [P, PACK, P], U32)
+        nc.vector.tensor_copy(tab_g[:].rearrange("k t p -> k p t"), tab_pool[:].bitcast(U32).indirect(offsets[:]))
+
+        mean_sq = alloc("mean_sq", [P, BLOCKS, G], F32)
+        zh = []
+        for b in range(BLOCKS):
+            w_grouped = alloc(f"w_grouped{b}", [P, P, PACK], BF16)
+            cols = slice((b % 2) * P, (b % 2 + 1) * P)
+            nc.vector.tensor_copy(out=w_grouped[:], in_=w_raw[b // 2][:, :, cols].rearrange("p j r -> p r j"))
+            w_codes, w_scales = quantize(f"w{b}", w_grouped[:].rearrange("p r j -> p (r j)"), P)
+            bank = ps.tile([P, PACK, P], F32, name=f"zh{b}", tag=f"bank_z{b}")
+            for t in range(PACK):
+                nc.tensor.matmul_mx(
+                    out=bank[:, t, :], lhsT=tab_g[:, t, :].bitcast(FP8X4), lhsT_scale=tab_gs[:, t, :],
+                    rhs=w_codes[:].bitcast(FP8X4), rhs_scale=w_scales[:], start=True, stop=True,
+                )
+            zh.append(bank)
+            squares = alloc(f"squares{b}", [P, PACK, P], F32)
+            nc.scalar.activation(squares[:], bank[:], ACT.Square)
+            sums = ps.tile([P, P], F32, name=f"sums{b}", tag="bank_s", bufs=2)
+            for t in range(PACK):
+                nc.tensor.matmul(
+                    sums[:], lhsT=squares[:, t, :], rhs=ident[:], is_transpose=True,
+                    start=(t == 0), stop=(t == PACK - 1),
+                )
+            nc.vector.tensor_reduce(
+                out=mean_sq[:, b, :], in_=sums[:].rearrange("r (g e) -> r g e", g=G), axis=AX.X, op=ALU.add
+            )
+            if b == 0:
+                weights = alloc("weights", [P, PACK, P], F32)
+                row_sum = alloc("row_sum", [P, 1], F32)
+                nc.vector.scalar_tensor_tensor(
+                    out=weights[:], in0=scores_dealt, scalar=th_col[:], in1=soft[:],
+                    op0=ALU.subtract, op1=ALU.max, accum_out=row_sum[:],
+                )
+                total = alloc("total", [P, 1], F32)
+                nc.vector.tensor_tensor(total[:], row_sum[:], reserve_col[:], ALU.add)
+                inv_total = alloc("inv_total", [P, 1], F32)
+                nc.vector.reciprocal(inv_total[:], total[:])
+                shares = alloc("shares", [P, PACK, P], F32)
+                nc.vector.tensor_scalar(shares[:], weights[:], inv_total[:], None, ALU.mult)
+                shares_t = ps.tile([P, PACK, Q], F32, name="shares_t", tag="bank_w")
+                for t in range(PACK):
+                    nc.tensor.transpose(shares_t[:, t, :], shares[:, t, :], ident[:])
+                wt_grouped = alloc("wt_grouped", [P, Q, PACK], BF16)
+                nc.vector.tensor_tensor(
+                    wt_grouped[:], shares_t[:].rearrange("p t q -> p q t"),
+                    os_cols[:].unsqueeze(1).to_broadcast([P, Q, PACK]), ALU.mult,
+                )
+                wt_codes, wt_scales = quantize("wt", wt_grouped[:].rearrange("p q t -> p (q t)"), Q)
+
+        inv_rms = alloc("inv_rms", [P, BLOCKS, G], F32)
+        nc.scalar.activation(inv_rms[:], mean_sq[:], ACT.Abs_reciprocal_sqrt, bias=0.1, scale=1.0 / PAGE)
+
+        normed = []
+        for b in range(BLOCKS):
+            factor = alloc(f"factor{b}", [P, G, PACK], F32)
+            nc.vector.tensor_scalar(
+                factor[:], inv_rms[:, b, :].unsqueeze(2).to_broadcast([P, G, PACK]),
+                gain_cols[:, b : b + 1], None, ALU.mult,
+            )
+            factor_ps = ps.tile([P, P], F32, name=f"factor_ps{b}", tag="bank_s", bufs=2)
+            nc.tensor.transpose(factor_ps[:], factor[:].rearrange("r g e -> r (g e)"), ident[:])
+            factor_t = alloc(f"factor_t{b}", [P, P], F32)
+            nc.vector.tensor_copy(factor_t[:], factor_ps[:])
+            pre = alloc(f"pre{b}", [P, P, PACK], F32)
+            nc.vector.tensor_tensor(
+                pre[:], zh[b][:].rearrange("p t r -> p r t"),
+                factor_t[:].unsqueeze(2).to_broadcast([P, P, PACK]), ALU.mult,
+            )
+            normed.append(pre)
+
+        for b in range(BLOCKS):
+            hv = alloc(f"hv{b}", [P, P, PACK], F32)
+            nc.scalar.activation(hv[:], normed[b][:], ACT.Silu)
+            ht_grouped = alloc(f"ht_grouped{b}", [P, P, PACK], BF16)
+            nc.vector.tensor_tensor(
+                ht_grouped[:], hv[:], vs_cols[:].unsqueeze(1).to_broadcast([P, P, PACK]), ALU.mult
+            )
+            ht_codes, ht_scales = quantize(f"ht{b}", ht_grouped[:].rearrange("p r t -> p (r t)"), P)
+            acc = ps.tile([Q, P], F32, name=f"acc{b}", tag=("bank_a", "bank_w")[b % 2])
+            nc.tensor.matmul_mx(
+                out=acc[:], lhsT=wt_codes[:].bitcast(FP8X4), lhsT_scale=wt_scales[:],
+                rhs=ht_codes[:].bitcast(FP8X4), rhs_scale=ht_scales[:], start=True, stop=True,
+            )
+            result = alloc(f"result{b}", [Q, P], F32)
+            nc.scalar.copy(result[:], acc[:])
+            nc.sync.dma_start(out=out[:, b * P : (b + 1) * P], in_=result[:])

@@ -22,6 +22,7 @@ PACK = 4
 BLOCKS = R // P
 PAGE = I // G
 EXP_CAP = 2.0**40
+GPSIMD_FEATURES = 192
 
 
 def tile_attend_lrscaled_capped_kernel(
@@ -32,52 +33,68 @@ def tile_attend_lrscaled_capped_kernel(
         sb = ctx.enter_context(tc.tile_pool(name="sb", bufs=1))
         ps = ctx.enter_context(tc.psum_pool(name="ps", bufs=1))
 
-        def alloc(name, shape, dtype):
-            return sb.tile(shape, dtype, name=name, align_bytes=64)
+        def alloc(name, shape, dtype, tag=""):
+            return sb.tile(shape, dtype, name=name, tag=tag or name, align_bytes=64)
 
-        def quantize(name, grouped, width):
-            codes = alloc(name + "_codes", [P, width], U32)
+        def quantize(name, grouped, width, tag=""):
+            codes = alloc(name + "_codes", [P, width], U32, tag=tag)
             scales = alloc(name + "_scales", [P, width], U8)
             nc.vector.quantize_mx(out=codes[:].bitcast(FP8X4), scales=scales[:], in_=grouped)
             return codes, scales
 
+        def interleave(copy, grouped, raw):
+            copy(
+                out=grouped[:].rearrange("p (c i) j -> p c j i", i=4),
+                in_=raw.rearrange("p j (c i) -> p c j i", i=4),
+            )
+
         def load_scale_rows(queue, pool_tile, scales_hbm, j):
             queue.dma_start(out=pool_tile[j:P:32, :].bitcast(I32), in_=scales_hbm[0, j:16:4, :].bitcast(I32))
 
-        keys_bytes = alloc("keys_bytes", [P, T], U8)
-        nc.gpsimd.memset(keys_bytes[:].bitcast(I32), 0)
-        tab_bytes = alloc("tab_bytes", [P, T], U8)
-        nc.vector.memset(tab_bytes[:].bitcast(I32), 0)
-        for j in range(4):
-            load_scale_rows(nc.scalar if j < 3 else nc.gpsimd, keys_bytes, keys_scales, j)
-        for j in range(4):
-            load_scale_rows(nc.gpsimd, tab_bytes, tab_scales, j)
+        def load_words(pool_words, words_hbm, cols):
+            words = words_hbm[0].rearrange("p n t -> p (n t)").bitcast(I32)
+            nc.sync.dma_start(out=pool_words[:, cols], in_=words[:, cols])
+
+        def load_scales(name, scales_hbm, clear, queues):
+            pool_bytes = alloc(name, [P, T], U8)
+            clear.memset(pool_bytes[:].bitcast(I32), 0)
+            for j in range(4):
+                load_scale_rows(queues[j % len(queues)], pool_bytes, scales_hbm, j)
+            return pool_bytes
+
+        w1_rows = w1.rearrange("(p j) r -> p j r", j=PACK)
+
+        def load_w1(first, count):
+            raw = alloc(f"w_raw{first}", [P, PACK, count * P], F32)
+            nc.sync.dma_start(out=raw[:], in_=w1_rows[:, :, first * P : (first + count) * P])
+            return [raw[:, :, n * P : (n + 1) * P] for n in range(count)]
+
         th_col = alloc("th_col", [P, 1], F32)
         nc.scalar.dma_start(out=th_col[:], in_=th)
-
         offsets = alloc("offsets", [P, I // 16], U16)
         nc.sync.dma_start(offsets[:], offs)
+        keys_pool = alloc("keys_pool", [P, T], I32)
+        load_words(keys_pool, keys_words, slice(0, T // 4))
+        keys_bytes = load_scales("keys_bytes", keys_scales, nc.gpsimd, (nc.scalar, nc.sync))
+        load_words(keys_pool, keys_words, slice(T // 4, T))
         q_raw = alloc("q_raw", [P, PACK, Q], F32)
         nc.sync.dma_start(out=q_raw[:], in_=query.rearrange("(p j) q -> p j q", j=PACK))
-        keys_pool = alloc("keys_pool", [P, T], I32)
-        nc.sync.dma_start(out=keys_pool[:], in_=keys_words[0].rearrange("p n t -> p (n t)").bitcast(I32))
+        tab_bytes = load_scales("tab_bytes", tab_scales, nc.vector, (nc.sync,))
+        w_raw = load_w1(0, 1)
         tab_pool = alloc("tab_pool", [P, T], I32)
-        nc.sync.dma_start(out=tab_pool[:], in_=tab_words[0].rearrange("p n t -> p (n t)").bitcast(I32))
-        w1_rows = w1.rearrange("(p j) r -> p j r", j=PACK)
-        w_raw = []
-        for h in range(2):
-            half = alloc(f"w_raw{h}", [P, PACK, 2 * P], F32)
-            nc.sync.dma_start(out=half[:], in_=w1_rows[:, :, 2 * P * h : 2 * P * (h + 1)])
-            w_raw.append(half)
+        load_words(tab_pool, tab_words, slice(0, T))
+        w_raw = w_raw + load_w1(1, 1) + load_w1(2, 2)
+
         reserve_col = alloc("reserve_col", [P, 1], F32)
         nc.sync.dma_start(out=reserve_col[:], in_=reserve)
-        os_cols = alloc("os_cols", [P, PACK], F32)
-        nc.sync.dma_start(out=os_cols[:], in_=slot_os.rearrange("o (p t) -> p (o t)", t=PACK))
-        vs_cols = alloc("vs_cols", [P, PACK], F32)
-        nc.sync.dma_start(out=vs_cols[:], in_=slot_vs.rearrange("o (p t) -> p (o t)", t=PACK))
-        gain_cols = alloc("gain_cols", [P, BLOCKS], F32)
-        with nc.allow_non_contiguous_dma(reason="one gain a partition for each block of hidden features"):
-            nc.sync.dma_start(out=gain_cols[:], in_=gain.rearrange("(b p) o -> p (b o)", p=P))
+        rows = alloc("rows", [P, P], F32)
+        nc.gpsimd.memset(rows[:], 0.0)
+        for first, vec in ((0, slot_os), (4, slot_vs)):
+            nc.sync.dma_start(
+                out=rows[first : first + PACK, :].rearrange("t (c e) -> t c e", e=PACK),
+                in_=vec.rearrange("o (c t e) -> t (o c) e", t=PACK, e=PACK),
+            )
+        nc.sync.dma_start(out=rows[8:12, :], in_=gain.rearrange("(b p) o -> b (p o)", p=P))
 
         ident = alloc("ident", [P, P], F32)
         make_identity(nc, ident[:])
@@ -85,36 +102,40 @@ def tile_attend_lrscaled_capped_kernel(
         neg_th = alloc("neg_th", [P, 1], F32)
         nc.scalar.mul(neg_th[:], th_col[:], -1.0)
         q_grouped = alloc("q_grouped", [P, Q, PACK], BF16)
-        nc.vector.tensor_copy(out=q_grouped[:], in_=q_raw[:].rearrange("p j q -> p q j"))
+        interleave(nc.scalar.copy, q_grouped, q_raw[:])
         keys_gs = alloc("keys_gs", [P, I], U8)
         nc.vector.tensor_copy(keys_gs[:], keys_bytes[:].indirect(offsets[:]))
-        q_codes, q_scales = quantize("q", q_grouped[:].rearrange("p q j -> p (q j)"), Q)
         keys_g = alloc("keys_g", [P, I], U32)
         nc.vector.tensor_copy(keys_g[:], keys_pool[:].bitcast(U32).indirect(offsets[:]))
+        q_codes, q_scales = quantize("q", q_grouped[:].rearrange("p q j -> p (q j)"), Q)
         scores = ps.tile([P, I], F32, name="scores", tag="bank_a")
         nc.tensor.matmul_mx(
             out=scores[:], lhsT=q_codes[:].bitcast(FP8X4), lhsT_scale=q_scales[:],
             rhs=keys_g[:].bitcast(FP8X4), rhs_scale=keys_gs[:], start=True, stop=True,
         )
-        scores_dealt = scores[:].rearrange("q (p t) -> q t p", t=PACK)
-        expx = alloc("expx", [P, PACK, P], F32)
-        nc.scalar.activation(expx[:], scores_dealt, ACT.Exp, bias=neg_th[:])
-        capped = alloc("capped", [P, PACK, P], F32)
+        expx = alloc("expx", [P, I], F32)
+        nc.scalar.activation(expx[:], scores[:], ACT.Exp, bias=neg_th[:])
+        capped = alloc("capped", [P, I], F32)
         nc.gpsimd.tensor_scalar(capped[:], expx[:], EXP_CAP, 0.0, ALU.min, ALU.max)
-        soft = alloc("soft", [P, PACK, P], F32)
+        soft = alloc("soft", [P, I], F32)
         nc.scalar.activation(soft[:], capped[:], ACT.Ln, bias=1.0)
 
+        tab_gs_listed = alloc("tab_gs_listed", [P, I], U8)
+        nc.vector.tensor_copy(tab_gs_listed[:], tab_bytes[:].indirect(offsets[:]))
         tab_gs = alloc("tab_gs", [P, PACK, P], U8)
-        nc.vector.tensor_copy(tab_gs[:].rearrange("k t p -> k p t"), tab_bytes[:].indirect(offsets[:]))
+        nc.vector.tensor_copy(
+            tab_gs[:].rearrange("k t p -> k (t p)").bitcast(I32).rearrange("k (t c) -> k t c", t=PACK),
+            tab_gs_listed[:].bitcast(I32).rearrange("k (c t) -> k t c", t=PACK),
+        )
         tab_g = alloc("tab_g", [P, PACK, P], U32)
-        nc.vector.tensor_copy(tab_g[:].rearrange("k t p -> k p t"), tab_pool[:].bitcast(U32).indirect(offsets[:]))
+        nc.vector.tensor_copy(
+            tab_g[:].rearrange("k t (c e) -> k c t e", e=PACK), tab_pool[:].bitcast(U32).indirect(offsets[:])
+        )
 
-        mean_sq = alloc("mean_sq", [P, BLOCKS, G], F32)
-        zh = []
+        zh, squares = [], []
         for b in range(BLOCKS):
             w_grouped = alloc(f"w_grouped{b}", [P, P, PACK], BF16)
-            cols = slice((b % 2) * P, (b % 2 + 1) * P)
-            nc.vector.tensor_copy(out=w_grouped[:], in_=w_raw[b // 2][:, :, cols].rearrange("p j r -> p r j"))
+            interleave(nc.vector.tensor_copy, w_grouped, w_raw[b])
             w_codes, w_scales = quantize(f"w{b}", w_grouped[:].rearrange("p r j -> p (r j)"), P)
             bank = ps.tile([P, PACK, P], F32, name=f"zh{b}", tag=f"bank_z{b}")
             for t in range(PACK):
@@ -123,70 +144,110 @@ def tile_attend_lrscaled_capped_kernel(
                     rhs=w_codes[:].bitcast(FP8X4), rhs_scale=w_scales[:], start=True, stop=True,
                 )
             zh.append(bank)
-            squares = alloc(f"squares{b}", [P, PACK, P], F32)
-            nc.scalar.activation(squares[:], bank[:], ACT.Square)
-            sums = ps.tile([P, P], F32, name=f"sums{b}", tag="bank_s", bufs=2)
+            square = alloc(f"squares{b}", [P, PACK, P], F32)
+            nc.scalar.activation(square[:], bank[:], ACT.Square)
+            squares.append(square)
+
+        weights = alloc("weights", [P, I], F32, tag=f"w_grouped{BLOCKS - 1}")
+        row_sum = alloc("row_sum", [P, 1], F32)
+        nc.vector.scalar_tensor_tensor(
+            out=weights[:], in0=scores[:], scalar=th_col[:], in1=soft[:],
+            op0=ALU.subtract, op1=ALU.max, accum_out=row_sum[:],
+        )
+
+        sums = ps.tile([P, BLOCKS, P], F32, name="sums", tag="bank_a")
+        for b in range(BLOCKS):
             for t in range(PACK):
                 nc.tensor.matmul(
-                    sums[:], lhsT=squares[:, t, :], rhs=ident[:], is_transpose=True,
+                    sums[:, b, :], lhsT=squares[b][:, t, :], rhs=ident[:], is_transpose=True,
                     start=(t == 0), stop=(t == PACK - 1),
                 )
-            nc.vector.tensor_reduce(
-                out=mean_sq[:, b, :], in_=sums[:].rearrange("r (g e) -> r g e", g=G), axis=AX.X, op=ALU.add
-            )
-            if b == 0:
-                weights = alloc("weights", [P, PACK, P], F32)
-                row_sum = alloc("row_sum", [P, 1], F32)
-                nc.vector.scalar_tensor_tensor(
-                    out=weights[:], in0=scores_dealt, scalar=th_col[:], in1=soft[:],
-                    op0=ALU.subtract, op1=ALU.max, accum_out=row_sum[:],
-                )
-                total = alloc("total", [P, 1], F32)
-                nc.vector.tensor_tensor(total[:], row_sum[:], reserve_col[:], ALU.add)
-                inv_total = alloc("inv_total", [P, 1], F32)
-                nc.vector.reciprocal(inv_total[:], total[:])
-                shares = alloc("shares", [P, PACK, P], F32)
-                nc.vector.tensor_scalar(shares[:], weights[:], inv_total[:], None, ALU.mult)
-                shares_t = ps.tile([P, PACK, Q], F32, name="shares_t", tag="bank_w")
-                for t in range(PACK):
-                    nc.tensor.transpose(shares_t[:, t, :], shares[:, t, :], ident[:])
-                wt_grouped = alloc("wt_grouped", [P, Q, PACK], BF16)
-                nc.vector.tensor_tensor(
-                    wt_grouped[:], shares_t[:].rearrange("p t q -> p q t"),
-                    os_cols[:].unsqueeze(1).to_broadcast([P, Q, PACK]), ALU.mult,
-                )
-                wt_codes, wt_scales = quantize("wt", wt_grouped[:].rearrange("p q t -> p (q t)"), Q)
-
+        mean_sq = alloc("mean_sq", [P, BLOCKS * G], F32)
+        nc.vector.tensor_reduce(
+            out=mean_sq[:], in_=sums[:].rearrange("r b (g e) -> r (b g) e", g=G), axis=AX.X, op=ALU.add
+        )
         inv_rms = alloc("inv_rms", [P, BLOCKS, G], F32)
-        nc.scalar.activation(inv_rms[:], mean_sq[:], ACT.Abs_reciprocal_sqrt, bias=0.1, scale=1.0 / PAGE)
+        nc.scalar.activation(
+            inv_rms[:].rearrange("r b g -> r (b g)"), mean_sq[:], ACT.Abs_reciprocal_sqrt, bias=0.1, scale=1.0 / PAGE
+        )
 
-        normed = []
-        for b in range(BLOCKS):
+        total = alloc("total", [P, 1], F32)
+        nc.vector.tensor_tensor(total[:], row_sum[:], reserve_col[:], ALU.add)
+        inv_total = alloc("inv_total", [P, 1], F32)
+        nc.vector.reciprocal(inv_total[:], total[:])
+        shares = alloc("shares", [P, PACK, P], F32)
+        nc.vector.tensor_scalar(
+            shares[:].rearrange("q t (c e) -> q t c e", e=PACK),
+            weights[:].rearrange("q (c t e) -> q t c e", t=PACK, e=PACK), inv_total[:], None, ALU.mult,
+        )
+        shares_t = ps.tile([P, PACK, Q], F32, name="shares_t", tag="bank_w")
+        for t in range(PACK):
+            nc.tensor.transpose(shares_t[:, t, :], shares[:, t, :], ident[:])
+        cols_ps = ps.tile([P, P], F32, name="cols_ps", tag="bank_v")
+        nc.tensor.transpose(cols_ps[:], rows[:], ident[:])
+        columns = alloc("columns", [P, 12], F32)
+        nc.vector.tensor_copy(columns[:], cols_ps[:, :12])
+        os_cols, vs_cols, gain_cols = columns[:, 0:4], columns[:, 4:8], columns[:, 8:12]
+
+        wt_grouped = alloc("wt_grouped", [P, Q, PACK], BF16)
+        nc.vector.tensor_tensor(
+            wt_grouped[:], shares_t[:].rearrange("p t q -> p q t"),
+            os_cols.unsqueeze(1).to_broadcast([P, Q, PACK]), ALU.mult,
+        )
+        wt_codes, wt_scales = quantize("wt", wt_grouped[:].rearrange("p q t -> p (q t)"), Q)
+
+        zh0_grouped = alloc("zh0_grouped", [P, P, PACK], F32, tag="soft")
+        nc.vector.tensor_copy(zh0_grouped[:], zh[0][:].rearrange("p t r -> p r t"))
+
+        def turn_factor(b):
             factor = alloc(f"factor{b}", [P, G, PACK], F32)
-            nc.vector.tensor_scalar(
+            nc.gpsimd.tensor_scalar(
                 factor[:], inv_rms[:, b, :].unsqueeze(2).to_broadcast([P, G, PACK]),
-                gain_cols[:, b : b + 1], None, ALU.mult,
+                gain_cols[:, b : b + 1], 0.0, ALU.mult, ALU.add,
             )
-            factor_ps = ps.tile([P, P], F32, name=f"factor_ps{b}", tag="bank_s", bufs=2)
+            factor_ps = ps.tile([P, P], F32, name=f"factor_ps{b}", tag=("bank_s", "bank_a")[b % 2])
             nc.tensor.transpose(factor_ps[:], factor[:].rearrange("r g e -> r (g e)"), ident[:])
+            if b == 0:
+                return factor_ps
             factor_t = alloc(f"factor_t{b}", [P, P], F32)
             nc.vector.tensor_copy(factor_t[:], factor_ps[:])
+            return factor_t
+
+        normed = []
+        factors = []
+        for b in range(BLOCKS):
+            while len(factors) < min(BLOCKS, 2 * b + 1, b + 2):
+                factors.append(turn_factor(len(factors)))
             pre = alloc(f"pre{b}", [P, P, PACK], F32)
             nc.vector.tensor_tensor(
-                pre[:], zh[b][:].rearrange("p t r -> p r t"),
-                factor_t[:].unsqueeze(2).to_broadcast([P, P, PACK]), ALU.mult,
+                pre[:], zh0_grouped[:] if b == 0 else zh[b][:].rearrange("p t r -> p r t"),
+                factors[b][:].unsqueeze(2).to_broadcast([P, P, PACK]), ALU.mult,
             )
             normed.append(pre)
 
+        grouped = []
         for b in range(BLOCKS):
             hv = alloc(f"hv{b}", [P, P, PACK], F32)
             nc.scalar.activation(hv[:], normed[b][:], ACT.Silu)
             ht_grouped = alloc(f"ht_grouped{b}", [P, P, PACK], BF16)
-            nc.vector.tensor_tensor(
-                ht_grouped[:], hv[:], vs_cols[:].unsqueeze(1).to_broadcast([P, P, PACK]), ALU.mult
+            split = min(P, max(0, GPSIMD_FEATURES - b * P))
+            for engine, value_scale, feats in (
+                (nc.gpsimd, vs_cols, slice(0, split)),
+                (nc.vector, cols_ps[:, 4:8], slice(split, P)),
+            ):
+                width = feats.stop - feats.start
+                if width:
+                    engine.tensor_tensor(
+                        ht_grouped[:, feats, :], hv[:, feats, :],
+                        value_scale.unsqueeze(1).to_broadcast([P, width, PACK]), ALU.mult,
+                    )
+            grouped.append(ht_grouped)
+
+        for b in range(BLOCKS):
+            ht_codes, ht_scales = quantize(
+                f"ht{b}", grouped[b][:].rearrange("p r t -> p (r t)"), P, tag="hv2" if b == 0 else ""
             )
-            ht_codes, ht_scales = quantize(f"ht{b}", ht_grouped[:].rearrange("p r t -> p (r t)"), P)
-            acc = ps.tile([Q, P], F32, name=f"acc{b}", tag=("bank_a", "bank_w")[b % 2])
+            acc = ps.tile([Q, P], F32, name=f"acc{b}", tag=f"bank_z{b}")
             nc.tensor.matmul_mx(
                 out=acc[:], lhsT=wt_codes[:].bitcast(FP8X4), lhsT_scale=wt_scales[:],
                 rhs=ht_codes[:].bitcast(FP8X4), rhs_scale=ht_scales[:], start=True, stop=True,

@@ -80,10 +80,9 @@ def tile_attend_lrscaled_capped_kernel(
         q_raw = alloc("q_raw", [P, PACK, Q], F32)
         nc.sync.dma_start(out=q_raw[:], in_=query.rearrange("(p j) q -> p j q", j=PACK))
         tab_bytes = load_scales("tab_bytes", tab_scales, nc.vector, (nc.sync,))
-        w_raw = load_w1(0, 1)
         tab_pool = alloc("tab_pool", [P, T], I32)
         load_words(tab_pool, tab_words, slice(0, T))
-        w_raw = w_raw + load_w1(1, 1) + load_w1(2, 2)
+        w_raw = load_w1(0, 2) + load_w1(2, 2)
 
         reserve_col = alloc("reserve_col", [P, 1], F32)
         nc.sync.dma_start(out=reserve_col[:], in_=reserve)
@@ -155,17 +154,19 @@ def tile_attend_lrscaled_capped_kernel(
             op0=ALU.subtract, op1=ALU.max, accum_out=row_sum[:],
         )
 
-        sums = ps.tile([P, BLOCKS, P], F32, name="sums", tag="bank_a")
-        for b in range(BLOCKS):
-            for t in range(PACK):
-                nc.tensor.matmul(
-                    sums[:, b, :], lhsT=squares[b][:, t, :], rhs=ident[:], is_transpose=True,
-                    start=(t == 0), stop=(t == PACK - 1),
-                )
         mean_sq = alloc("mean_sq", [P, BLOCKS * G], F32)
-        nc.vector.tensor_reduce(
-            out=mean_sq[:], in_=sums[:].rearrange("r b (g e) -> r (b g) e", g=G), axis=AX.X, op=ALU.add
-        )
+        for first, count, tag in ((0, BLOCKS - 1, "bank_a"), (BLOCKS - 1, 1, "bank_s")):
+            sums = ps.tile([P, count, P], F32, name=f"sums{first}", tag=tag)
+            for n in range(count):
+                for t in range(PACK):
+                    nc.tensor.matmul(
+                        sums[:, n, :], lhsT=squares[first + n][:, t, :], rhs=ident[:], is_transpose=True,
+                        start=(t == 0), stop=(t == PACK - 1),
+                    )
+            nc.vector.tensor_reduce(
+                out=mean_sq[:, first * G : (first + count) * G],
+                in_=sums[:].rearrange("r b (g e) -> r (b g) e", g=G), axis=AX.X, op=ALU.add,
+            )
         inv_rms = alloc("inv_rms", [P, BLOCKS, G], F32)
         nc.scalar.activation(
             inv_rms[:].rearrange("r b g -> r (b g)"), mean_sq[:], ACT.Abs_reciprocal_sqrt, bias=0.1, scale=1.0 / PAGE

@@ -19,10 +19,18 @@ AX = mybir.AxisListType
 
 P = 128
 PACK = 4
+RUN = 4
+LINE = 4
+QUADRANT = 32
+SCALE_ROWS = 4
 BLOCKS = R // P
+LAST = BLOCKS - 1
 PAGE = I // G
+RMS_EPS = 0.1
 EXP_CAP = 2.0**40
+KEYS_FIRST = T // 4
 GPSIMD_FEATURES = 192
+OS_AT, VS_AT, GAIN_AT, SMALL = 0, PACK, 2 * PACK, 2 * PACK + BLOCKS
 
 
 def tile_attend_lrscaled_capped_kernel(
@@ -44,12 +52,9 @@ def tile_attend_lrscaled_capped_kernel(
 
         def interleave(copy, grouped, raw):
             copy(
-                out=grouped[:].rearrange("p (c i) j -> p c j i", i=4),
-                in_=raw.rearrange("p j (c i) -> p c j i", i=4),
+                out=grouped[:].rearrange("p (c i) j -> p c j i", i=LINE),
+                in_=raw.rearrange("p j (c i) -> p c j i", i=LINE),
             )
-
-        def load_scale_rows(queue, pool_tile, scales_hbm, j):
-            queue.dma_start(out=pool_tile[j:P:32, :].bitcast(I32), in_=scales_hbm[0, j:16:4, :].bitcast(I32))
 
         def load_words(pool_words, words_hbm, cols):
             words = words_hbm[0].rearrange("p n t -> p (n t)").bitcast(I32)
@@ -58,8 +63,11 @@ def tile_attend_lrscaled_capped_kernel(
         def load_scales(name, scales_hbm, clear, queues):
             pool_bytes = alloc(name, [P, T], U8)
             clear.memset(pool_bytes[:].bitcast(I32), 0)
-            for j in range(4):
-                load_scale_rows(queues[j % len(queues)], pool_bytes, scales_hbm, j)
+            for j in range(SCALE_ROWS):
+                queues[j % len(queues)].dma_start(
+                    out=pool_bytes[j:P:QUADRANT, :].bitcast(I32),
+                    in_=scales_hbm[0, j : D // QUADRANT : SCALE_ROWS, :].bitcast(I32),
+                )
             return pool_bytes
 
         w1_rows = w1.rearrange("(p j) r -> p j r", j=PACK)
@@ -74,26 +82,26 @@ def tile_attend_lrscaled_capped_kernel(
         offsets = alloc("offsets", [P, I // 16], U16)
         nc.sync.dma_start(offsets[:], offs)
         keys_pool = alloc("keys_pool", [P, T], I32)
-        load_words(keys_pool, keys_words, slice(0, T // 4))
+        load_words(keys_pool, keys_words, slice(0, KEYS_FIRST))
         keys_bytes = load_scales("keys_bytes", keys_scales, nc.gpsimd, (nc.scalar, nc.sync))
-        load_words(keys_pool, keys_words, slice(T // 4, T))
+        load_words(keys_pool, keys_words, slice(KEYS_FIRST, T))
         q_raw = alloc("q_raw", [P, PACK, Q], F32)
         nc.sync.dma_start(out=q_raw[:], in_=query.rearrange("(p j) q -> p j q", j=PACK))
         tab_bytes = load_scales("tab_bytes", tab_scales, nc.vector, (nc.sync,))
         tab_pool = alloc("tab_pool", [P, T], I32)
         load_words(tab_pool, tab_words, slice(0, T))
-        w_raw = load_w1(0, 2) + load_w1(2, 2)
+        w_raw = load_w1(0, BLOCKS // 2) + load_w1(BLOCKS // 2, BLOCKS // 2)
 
         reserve_col = alloc("reserve_col", [P, 1], F32)
         nc.sync.dma_start(out=reserve_col[:], in_=reserve)
         rows = alloc("rows", [P, P], F32)
         nc.gpsimd.memset(rows[:], 0.0)
-        for first, vec in ((0, slot_os), (4, slot_vs)):
+        for first, vec in ((OS_AT, slot_os), (VS_AT, slot_vs)):
             nc.sync.dma_start(
-                out=rows[first : first + PACK, :].rearrange("t (c e) -> t c e", e=PACK),
-                in_=vec.rearrange("o (c t e) -> t (o c) e", t=PACK, e=PACK),
+                out=rows[first : first + PACK, :].rearrange("t (c e) -> t c e", e=RUN),
+                in_=vec.rearrange("o (c t e) -> t (o c) e", t=PACK, e=RUN),
             )
-        nc.sync.dma_start(out=rows[8:12, :], in_=gain.rearrange("(b p) o -> b (p o)", p=P))
+        nc.sync.dma_start(out=rows[GAIN_AT:SMALL, :], in_=gain.rearrange("(b p) o -> b (p o)", p=P))
 
         ident = alloc("ident", [P, P], F32)
         make_identity(nc, ident[:])
@@ -128,7 +136,7 @@ def tile_attend_lrscaled_capped_kernel(
         )
         tab_g = alloc("tab_g", [P, PACK, P], U32)
         nc.vector.tensor_copy(
-            tab_g[:].rearrange("k t (c e) -> k c t e", e=PACK), tab_pool[:].bitcast(U32).indirect(offsets[:])
+            tab_g[:].rearrange("k t (c e) -> k c t e", e=RUN), tab_pool[:].bitcast(U32).indirect(offsets[:])
         )
 
         zh, squares = [], []
@@ -147,15 +155,15 @@ def tile_attend_lrscaled_capped_kernel(
             nc.scalar.activation(square[:], bank[:], ACT.Square)
             squares.append(square)
 
-        weights = alloc("weights", [P, I], F32, tag=f"w_grouped{BLOCKS - 1}")
+        weights = alloc("weights", [P, I], F32, tag=f"w_grouped{LAST}")
         row_sum = alloc("row_sum", [P, 1], F32)
         nc.vector.scalar_tensor_tensor(
             out=weights[:], in0=scores[:], scalar=th_col[:], in1=soft[:],
             op0=ALU.subtract, op1=ALU.max, accum_out=row_sum[:],
         )
 
-        mean_sq = alloc("mean_sq", [P, BLOCKS * G], F32)
-        for first, count, tag in ((0, BLOCKS - 1, "bank_a"), (BLOCKS - 1, 1, "bank_s")):
+        page_sums = alloc("page_sums", [P, BLOCKS * G], F32)
+        for first, count, tag in ((0, LAST, "bank_a"), (LAST, 1, "bank_s")):
             sums = ps.tile([P, count, P], F32, name=f"sums{first}", tag=tag)
             for n in range(count):
                 for t in range(PACK):
@@ -164,12 +172,13 @@ def tile_attend_lrscaled_capped_kernel(
                         start=(t == 0), stop=(t == PACK - 1),
                     )
             nc.vector.tensor_reduce(
-                out=mean_sq[:, first * G : (first + count) * G],
+                out=page_sums[:, first * G : (first + count) * G],
                 in_=sums[:].rearrange("r b (g e) -> r (b g) e", g=G), axis=AX.X, op=ALU.add,
             )
         inv_rms = alloc("inv_rms", [P, BLOCKS, G], F32)
         nc.scalar.activation(
-            inv_rms[:].rearrange("r b g -> r (b g)"), mean_sq[:], ACT.Abs_reciprocal_sqrt, bias=0.1, scale=1.0 / PAGE
+            inv_rms[:].rearrange("r b g -> r (b g)"), page_sums[:], ACT.Abs_reciprocal_sqrt,
+            bias=RMS_EPS, scale=1.0 / PAGE,
         )
 
         total = alloc("total", [P, 1], F32)
@@ -178,17 +187,17 @@ def tile_attend_lrscaled_capped_kernel(
         nc.vector.reciprocal(inv_total[:], total[:])
         shares = alloc("shares", [P, PACK, P], F32)
         nc.vector.tensor_scalar(
-            shares[:].rearrange("q t (c e) -> q t c e", e=PACK),
-            weights[:].rearrange("q (c t e) -> q t c e", t=PACK, e=PACK), inv_total[:], None, ALU.mult,
+            shares[:].rearrange("q t (c e) -> q t c e", e=RUN),
+            weights[:].rearrange("q (c t e) -> q t c e", t=PACK, e=RUN), inv_total[:], None, ALU.mult,
         )
         shares_t = ps.tile([P, PACK, Q], F32, name="shares_t", tag="bank_w")
         for t in range(PACK):
             nc.tensor.transpose(shares_t[:, t, :], shares[:, t, :], ident[:])
         cols_ps = ps.tile([P, P], F32, name="cols_ps", tag="bank_v")
         nc.tensor.transpose(cols_ps[:], rows[:], ident[:])
-        columns = alloc("columns", [P, 12], F32)
-        nc.vector.tensor_copy(columns[:], cols_ps[:, :12])
-        os_cols, vs_cols, gain_cols = columns[:, 0:4], columns[:, 4:8], columns[:, 8:12]
+        columns = alloc("columns", [P, SMALL], F32)
+        nc.vector.tensor_copy(columns[:], cols_ps[:, :SMALL])
+        os_cols, vs_cols, gain_cols = columns[:, OS_AT:VS_AT], columns[:, VS_AT:GAIN_AT], columns[:, GAIN_AT:SMALL]
 
         wt_grouped = alloc("wt_grouped", [P, Q, PACK], BF16)
         nc.vector.tensor_tensor(
@@ -197,13 +206,15 @@ def tile_attend_lrscaled_capped_kernel(
         )
         wt_codes, wt_scales = quantize("wt", wt_grouped[:].rearrange("p q t -> p (q t)"), Q)
 
+        vs_grouped = alloc("vs_grouped", [P, P, PACK], F32)
+        nc.vector.tensor_copy(vs_grouped[:], vs_cols.unsqueeze(1).to_broadcast([P, P, PACK]))
         zh0_grouped = alloc("zh0_grouped", [P, P, PACK], F32, tag="soft")
         nc.vector.tensor_copy(zh0_grouped[:], zh[0][:].rearrange("p t r -> p r t"))
 
         def turn_factor(b):
-            factor = alloc(f"factor{b}", [P, G, PACK], F32)
+            factor = alloc(f"factor{b}", [P, G, RUN], F32)
             nc.gpsimd.tensor_scalar(
-                factor[:], inv_rms[:, b, :].unsqueeze(2).to_broadcast([P, G, PACK]),
+                factor[:], inv_rms[:, b, :].unsqueeze(2).to_broadcast([P, G, RUN]),
                 gain_cols[:, b : b + 1], 0.0, ALU.mult, ALU.add,
             )
             factor_ps = ps.tile([P, P], F32, name=f"factor_ps{b}", tag=("bank_s", "bank_a")[b % 2])
@@ -217,7 +228,8 @@ def tile_attend_lrscaled_capped_kernel(
         normed = []
         factors = []
         for b in range(BLOCKS):
-            while len(factors) < min(BLOCKS, 2 * b + 1, b + 2):
+            ahead = 0 if b == 0 else 1
+            while len(factors) < min(BLOCKS, b + 1 + ahead):
                 factors.append(turn_factor(len(factors)))
             pre = alloc(f"pre{b}", [P, P, PACK], F32)
             nc.vector.tensor_tensor(
@@ -232,21 +244,18 @@ def tile_attend_lrscaled_capped_kernel(
             nc.scalar.activation(hv[:], normed[b][:], ACT.Silu)
             ht_grouped = alloc(f"ht_grouped{b}", [P, P, PACK], BF16)
             split = min(P, max(0, GPSIMD_FEATURES - b * P))
-            for engine, value_scale, feats in (
-                (nc.gpsimd, vs_cols, slice(0, split)),
-                (nc.vector, cols_ps[:, 4:8], slice(split, P)),
-            ):
-                width = feats.stop - feats.start
-                if width:
-                    engine.tensor_tensor(
-                        ht_grouped[:, feats, :], hv[:, feats, :],
-                        value_scale.unsqueeze(1).to_broadcast([P, width, PACK]), ALU.mult,
-                    )
+            if split > 0:
+                nc.gpsimd.tensor_tensor(ht_grouped[:, :split, :], hv[:, :split, :], vs_grouped[:, :split, :], ALU.mult)
+            if split < P:
+                nc.vector.tensor_tensor(
+                    ht_grouped[:, split:, :], hv[:, split:, :],
+                    cols_ps[:, VS_AT:GAIN_AT].unsqueeze(1).to_broadcast([P, P - split, PACK]), ALU.mult,
+                )
             grouped.append(ht_grouped)
 
         for b in range(BLOCKS):
             ht_codes, ht_scales = quantize(
-                f"ht{b}", grouped[b][:].rearrange("p r t -> p (r t)"), P, tag="hv2" if b == 0 else ""
+                f"ht{b}", grouped[b][:].rearrange("p r t -> p (r t)"), P, tag=f"hv{LAST - 1}" if b == 0 else ""
             )
             acc = ps.tile([Q, P], F32, name=f"acc{b}", tag=f"bank_z{b}")
             nc.tensor.matmul_mx(

from contextlib import ExitStack

import concourse.mybir as mybir
from concourse.masks import make_identity

D, K, R, T, I, Q, G = 512, 512, 512, 2048, 512, 128, 32
FLOPS = 2 * (D * Q * I + K * R * I + I * Q * R)

F32 = mybir.dt.float32
BF16 = mybir.dt.bfloat16
I32 = mybir.dt.int32
U32 = mybir.dt.uint32
U16 = mybir.dt.uint16
U8 = mybir.dt.uint8
FP8X4 = mybir.dt.float8_e4m3fn_x4
ALU = mybir.AluOpType
ACT = mybir.ActivationFunctionType
AX = mybir.AxisListType

P = 128
PACK = 4
RUN = 4
LINE = 4
QUADRANT = 32
SCALE_ROWS = 4
BLOCKS = R // P
LAST = BLOCKS - 1
PAGE = I // G
RMS_EPS = 0.1
EXP_CAP = 2.0**40
KEYS_FIRST = T // 4
GPSIMD_FEATURES = 192
OS_AT, VS_AT, GAIN_AT, SMALL = 0, PACK, 2 * PACK, 2 * PACK + BLOCKS


def tile_attend_lrscaled_capped_kernel(
    tc, query, keys_words, keys_scales, th, reserve, tab_words, tab_scales, w1, gain, slot_os, slot_vs, offs, out
):
    nc = tc.nc
    with ExitStack() as ctx:
        sb = ctx.enter_context(tc.tile_pool(name="sb", bufs=1))
        ps = ctx.enter_context(tc.psum_pool(name="ps", bufs=1))

        def alloc(name, shape, dtype, tag=""):
            return sb.tile(shape, dtype, name=name, tag=tag or name, align_bytes=64)

        def quantize(name, grouped, width, tag=""):
            codes = alloc(name + "_codes", [P, width], U32, tag=tag)
            scales = alloc(name + "_scales", [P, width], U8)
            nc.vector.quantize_mx(out=codes[:].bitcast(FP8X4), scales=scales[:], in_=grouped)
            return codes, scales

        def interleave(copy, grouped, raw):
            copy(
                out=grouped[:].rearrange("p (c i) j -> p c j i", i=LINE),
                in_=raw.rearrange("p j (c i) -> p c j i", i=LINE),
            )

        def load_words(pool_words, words_hbm, cols):
            words = words_hbm[0].rearrange("p n t -> p (n t)").bitcast(I32)
            nc.sync.dma_start(out=pool_words[:, cols], in_=words[:, cols])

        def load_scales(name, scales_hbm, clear, queues):
            pool_bytes = alloc(name, [P, T], U8)
            clear.memset(pool_bytes[:].bitcast(I32), 0)
            for j in range(SCALE_ROWS):
                queues[j % len(queues)].dma_start(
                    out=pool_bytes[j:P:QUADRANT, :].bitcast(I32),
                    in_=scales_hbm[0, j : D // QUADRANT : SCALE_ROWS, :].bitcast(I32),
                )
            return pool_bytes

        w1_rows = w1.rearrange("(p j) r -> p j r", j=PACK)

        def load_w1(first, count):
            raw = alloc(f"w_raw{first}", [P, PACK, count * P], F32)
            nc.sync.dma_start(out=raw[:], in_=w1_rows[:, :, first * P : (first + count) * P])
            return [raw[:, :, n * P : (n + 1) * P] for n in range(count)]

        th_col = alloc("th_col", [P, 1], F32)
        nc.scalar.dma_start(out=th_col[:], in_=th)
        offsets = alloc("offsets", [P, I // 16], U16)
        nc.sync.dma_start(offsets[:], offs)
        keys_pool = alloc("keys_pool", [P, T], I32)
        load_words(keys_pool, keys_words, slice(0, KEYS_FIRST))
        keys_bytes = load_scales("keys_bytes", keys_scales, nc.gpsimd, (nc.scalar, nc.sync))
        load_words(keys_pool, keys_words, slice(KEYS_FIRST, T))
        q_raw = alloc("q_raw", [P, PACK, Q], F32)
        nc.sync.dma_start(out=q_raw[:], in_=query.rearrange("(p j) q -> p j q", j=PACK))
        tab_bytes = load_scales("tab_bytes", tab_scales, nc.vector, (nc.sync,))
        tab_pool = alloc("tab_pool", [P, T], I32)
        load_words(tab_pool, tab_words, slice(0, T))
        w_raw = load_w1(0, BLOCKS // 2) + load_w1(BLOCKS // 2, BLOCKS // 2)

        reserve_col = alloc("reserve_col", [P, 1], F32)
        nc.sync.dma_start(out=reserve_col[:], in_=reserve)
        rows = alloc("rows", [P, P], F32)
        nc.gpsimd.memset(rows[:], 0.0)
        for first, vec in ((OS_AT, slot_os), (VS_AT, slot_vs)):
            nc.sync.dma_start(
                out=rows[first : first + PACK, :].rearrange("t (c e) -> t c e", e=RUN),
                in_=vec.rearrange("o (c t e) -> t (o c) e", t=PACK, e=RUN),
            )
        nc.sync.dma_start(out=rows[GAIN_AT:SMALL, :], in_=gain.rearrange("(b p) o -> b (p o)", p=P))

        ident = alloc("ident", [P, P], F32)
        make_identity(nc, ident[:])

        neg_th = alloc("neg_th", [P, 1], F32)
        nc.scalar.mul(neg_th[:], th_col[:], -1.0)
        q_grouped = alloc("q_grouped", [P, Q, PACK], BF16)
        interleave(nc.scalar.copy, q_grouped, q_raw[:])
        keys_gs = alloc("keys_gs", [P, I], U8)
        nc.vector.tensor_copy(keys_gs[:], keys_bytes[:].indirect(offsets[:]))
        keys_g = alloc("keys_g", [P, I], U32)
        nc.vector.tensor_copy(keys_g[:], keys_pool[:].bitcast(U32).indirect(offsets[:]))
        q_codes, q_scales = quantize("q", q_grouped[:].rearrange("p q j -> p (q j)"), Q)
        scores = ps.tile([P, I], F32, name="scores", tag="bank_a")
        nc.tensor.matmul_mx(
            out=scores[:], lhsT=q_codes[:].bitcast(FP8X4), lhsT_scale=q_scales[:],
            rhs=keys_g[:].bitcast(FP8X4), rhs_scale=keys_gs[:], start=True, stop=True,
        )
        expx = alloc("expx", [P, I], F32)
        nc.scalar.activation(expx[:], scores[:], ACT.Exp, bias=neg_th[:])
        capped = alloc("capped", [P, I], F32)
        nc.gpsimd.tensor_scalar(capped[:], expx[:], EXP_CAP, 0.0, ALU.min, ALU.max)
        soft = alloc("soft", [P, I], F32)
        nc.scalar.activation(soft[:], capped[:], ACT.Ln, bias=1.0)

        tab_gs_listed = alloc("tab_gs_listed", [P, I], U8)
        nc.vector.tensor_copy(tab_gs_listed[:], tab_bytes[:].indirect(offsets[:]))
        tab_gs = alloc("tab_gs", [P, PACK, P], U8)
        nc.vector.tensor_copy(
            tab_gs[:].rearrange("k t p -> k (t p)").bitcast(I32).rearrange("k (t c) -> k t c", t=PACK),
            tab_gs_listed[:].bitcast(I32).rearrange("k (c t) -> k t c", t=PACK),
        )
        tab_g = alloc("tab_g", [P, PACK, P], U32)
        nc.vector.tensor_copy(
            tab_g[:].rearrange("k t (c e) -> k c t e", e=RUN), tab_pool[:].bitcast(U32).indirect(offsets[:])
        )

        zh, squares = [], []
        for b in range(BLOCKS):
            w_grouped = alloc(f"w_grouped{b}", [P, P, PACK], BF16)
            interleave(nc.vector.tensor_copy, w_grouped, w_raw[b])
            w_codes, w_scales = quantize(f"w{b}", w_grouped[:].rearrange("p r j -> p (r j)"), P)
            bank = ps.tile([P, PACK, P], F32, name=f"zh{b}", tag=f"bank_z{b}")
            for t in range(PACK):
                nc.tensor.matmul_mx(
                    out=bank[:, t, :], lhsT=tab_g[:, t, :].bitcast(FP8X4), lhsT_scale=tab_gs[:, t, :],
                    rhs=w_codes[:].bitcast(FP8X4), rhs_scale=w_scales[:], start=True, stop=True,
                )
            zh.append(bank)
            square = alloc(f"squares{b}", [P, PACK, P], F32)
            nc.scalar.activation(square[:], bank[:], ACT.Square)
            squares.append(square)

        weights = alloc("weights", [P, I], F32, tag=f"w_grouped{LAST}")
        row_sum = alloc("row_sum", [P, 1], F32)
        nc.vector.scalar_tensor_tensor(
            out=weights[:], in0=scores[:], scalar=th_col[:], in1=soft[:],
            op0=ALU.subtract, op1=ALU.max, accum_out=row_sum[:],
        )

        page_sums = alloc("page_sums", [P, BLOCKS * G], F32)
        for first, count, tag in ((0, LAST, "bank_a"), (LAST, 1, "bank_s")):
            sums = ps.tile([P, count, P], F32, name=f"sums{first}", tag=tag)
            for n in range(count):
                for t in range(PACK):
                    nc.tensor.matmul(
                        sums[:, n, :], lhsT=squares[first + n][:, t, :], rhs=ident[:], is_transpose=True,
                        start=(t == 0), stop=(t == PACK - 1),
                    )
            nc.vector.tensor_reduce(
                out=page_sums[:, first * G : (first + count) * G],
                in_=sums[:].rearrange("r b (g e) -> r (b g) e", g=G), axis=AX.X, op=ALU.add,
            )
        inv_rms = alloc("inv_rms", [P, BLOCKS, G], F32)
        nc.scalar.activation(
            inv_rms[:].rearrange("r b g -> r (b g)"), page_sums[:], ACT.Abs_reciprocal_sqrt,
            bias=RMS_EPS, scale=1.0 / PAGE,
        )

        total = alloc("total", [P, 1], F32)
        nc.vector.tensor_tensor(total[:], row_sum[:], reserve_col[:], ALU.add)
        inv_total = alloc("inv_total", [P, 1], F32)
        nc.vector.reciprocal(inv_total[:], total[:])
        shares = alloc("shares", [P, PACK, P], F32)
        nc.vector.tensor_scalar(
            shares[:].rearrange("q t (c e) -> q t c e", e=RUN),
            weights[:].rearrange("q (c t e) -> q t c e", t=PACK, e=RUN), inv_total[:], None, ALU.mult,
        )
        shares_t = ps.tile([P, PACK, Q], F32, name="shares_t", tag="bank_w")
        for t in range(PACK):
            nc.tensor.transpose(shares_t[:, t, :], shares[:, t, :], ident[:])
        cols_ps = ps.tile([P, P], F32, name="cols_ps", tag="bank_v")
        nc.tensor.transpose(cols_ps[:], rows[:], ident[:])
        columns = alloc("columns", [P, SMALL], F32)
        nc.vector.tensor_copy(columns[:], cols_ps[:, :SMALL])
        os_cols, vs_cols, gain_cols = columns[:, OS_AT:VS_AT], columns[:, VS_AT:GAIN_AT], columns[:, GAIN_AT:SMALL]

        wt_grouped = alloc("wt_grouped", [P, Q, PACK], BF16)
        nc.vector.tensor_tensor(
            wt_grouped[:], shares_t[:].rearrange("p t q -> p q t"),
            os_cols.unsqueeze(1).to_broadcast([P, Q, PACK]), ALU.mult,
        )
        wt_codes, wt_scales = quantize("wt", wt_grouped[:].rearrange("p q t -> p (q t)"), Q)

        vs_grouped = alloc("vs_grouped", [P, P, PACK], F32)
        nc.vector.tensor_copy(vs_grouped[:], vs_cols.unsqueeze(1).to_broadcast([P, P, PACK]))
        zh0_grouped = alloc("zh0_grouped", [P, P, PACK], F32, tag="soft")
        nc.vector.tensor_copy(zh0_grouped[:], zh[0][:].rearrange("p t r -> p r t"))

        def turn_factor(b):
            factor = alloc(f"factor{b}", [P, G, RUN], F32)
            nc.gpsimd.tensor_scalar(
                factor[:], inv_rms[:, b, :].unsqueeze(2).to_broadcast([P, G, RUN]),
                gain_cols[:, b : b + 1], 0.0, ALU.mult, ALU.add,
            )
            factor_ps = ps.tile([P, P], F32, name=f"factor_ps{b}", tag=("bank_s", "bank_a")[b % 2])
            nc.tensor.transpose(factor_ps[:], factor[:].rearrange("r g e -> r (g e)"), ident[:])
            if b == 0:
                return factor_ps
            factor_t = alloc(f"factor_t{b}", [P, P], F32)
            nc.vector.tensor_copy(factor_t[:], factor_ps[:])
            return factor_t

        normed = []
        factors = []
        for b in range(BLOCKS):
            ahead = 0 if b == 0 else 1
            while len(factors) < min(BLOCKS, b + 1 + ahead):
                factors.append(turn_factor(len(factors)))
            pre = alloc(f"pre{b}", [P, P, PACK], F32)
            nc.vector.tensor_tensor(
                pre[:], zh0_grouped[:] if b == 0 else zh[b][:].rearrange("p t r -> p r t"),
                factors[b][:].unsqueeze(2).to_broadcast([P, P, PACK]), ALU.mult,
            )
            normed.append(pre)

        grouped = []
        for b in range(BLOCKS):
            hv = alloc(f"hv{b}", [P, P, PACK], F32)
            nc.scalar.activation(hv[:], normed[b][:], ACT.Silu)
            ht_grouped = alloc(f"ht_grouped{b}", [P, P, PACK], BF16)
            split = min(P, max(0, GPSIMD_FEATURES - b * P))
            if split > 0:
                nc.gpsimd.tensor_tensor(ht_grouped[:, :split, :], hv[:, :split, :], vs_grouped[:, :split, :], ALU.mult)
            if split < P:
                nc.vector.tensor_tensor(
                    ht_grouped[:, split:, :], hv[:, split:, :],
                    cols_ps[:, VS_AT:GAIN_AT].unsqueeze(1).to_broadcast([P, P - split, PACK]), ALU.mult,
                )
            grouped.append(ht_grouped)

        for b in range(BLOCKS):
            ht_codes, ht_scales = quantize(
                f"ht{b}", grouped[b][:].rearrange("p r t -> p (r t)"), P, tag=f"hv{LAST - 1}" if b == 0 else ""
            )
            acc = ps.tile([Q, P], F32, name=f"acc{b}", tag=f"bank_z{b}")
            nc.tensor.matmul_mx(
                out=acc[:], lhsT=wt_codes[:].bitcast(FP8X4), lhsT_scale=wt_scales[:],
                rhs=ht_codes[:].bitcast(FP8X4), rhs_scale=ht_scales[:], start=True, stop=True,
            )
            result = alloc(f"result{b}", [Q, P], F32)
            nc.scalar.copy(result[:], acc[:])
            nc.sync.dma_start(out=out[:, b * P : (b + 1) * P], in_=result[:])
